import numpy as np
import ml_dtypes

BF16 = ml_dtypes.bfloat16


def bf(x):
    return np.asarray(x, np.float32).astype(BF16)


def f32(x):
    return np.asarray(x, np.float32)


def f64(x):
    return np.asarray(x).astype(np.float64)


def striped(idx):
    return np.tile(idx.reshape(-1, 16).T, (8, 1))


S, K, M, N = 512, 512, 128, 512


def setup_inputs():
    return {"base": bf(np.random.standard_normal((M, S))), "x": bf(np.random.standard_normal((K, N))), "w": bf(np.random.standard_normal((K, M)) / np.sqrt(K)), "offs": striped(np.random.permutation(S))}


def reference(base, x, w, offs):
    idx = offs[:16].T.reshape(-1)
    z = f64(base).copy()
    z[:, idx] += f64(w).T @ f64(x)
    return z

@@ -1,0 +1,49 @@
+import concourse.mybir as mybir
+from concourse.masks import make_identity
+
+BF16, F32, U16 = mybir.dt.bfloat16, mybir.dt.float32, mybir.dt.uint16
+
+P = 128
+S = 512
+N = 512
+K = 512
+KB = K // P
+
+FLOPS = 2 * K * P * N
+
+
+def tile_scatter_matmul_kernel(tc, base, x, w, offs, out):
+    nc = tc.nc
+    with (
+        tc.tile_pool(name="held", bufs=1) as held,
+        tc.psum_pool(name="psum", bufs=1) as psum,
+    ):
+        offsets = held.tile([P, N // 16], U16, name="offsets")
+        nc.sync.dma_start(offsets[:], offs)
+
+        base_sb = held.tile([P, S], BF16, name="base_sb")
+        nc.scalar.dma_start(base_sb[:], base)
+
+        w_sb = held.tile([P, KB, P], BF16, name="w_sb")
+        nc.scalar.dma_start(w_sb[:], w.rearrange("(a p) m -> p a m", p=P))
+        x_sb = held.tile([P, KB, N], BF16, name="x_sb")
+        nc.sync.dma_start(x_sb[:], x.rearrange("(a p) n -> p a n", p=P))
+
+        ident = held.tile([P, P], BF16, name="ident")
+        make_identity(nc, ident[:])
+
+        window = psum.tile([P, S], F32, name="window")
+        nc.tensor.matmul(window[:], ident[:], base_sb[:], start=True, stop=False)
+
+        for a in range(KB):
+            nc.tensor.matmul(
+                window[:].indirect(offsets[:]),
+                w_sb[:, a, :],
+                x_sb[:, a, :],
+                start=False,
+                stop=(a == KB - 1),
+            )
+
+        z_sb = held.tile([P, S], F32, name="z_sb")
+        nc.vector.tensor_copy(z_sb[:], window[:])
+        nc.sync.dma_start(out, z_sb[:])

@@ -18,16 +18,19 @@ def tile_scatter_matmul_kernel(tc, base, x, w, offs, out):
         tc.tile_pool(name="held", bufs=1) as held,
         tc.psum_pool(name="psum", bufs=1) as psum,
     ):
+        w_blocks = w.rearrange("(p a) m -> p a m", a=KB)
+        x_blocks = x.rearrange("(p a) n -> p a n", a=KB)
+
         offsets = held.tile([P, N // 16], U16, name="offsets")
         nc.sync.dma_start(offsets[:], offs)
-
         base_sb = held.tile([P, S], BF16, name="base_sb")
         nc.scalar.dma_start(base_sb[:], base)
-
         w_sb = held.tile([P, KB, P], BF16, name="w_sb")
-        nc.scalar.dma_start(w_sb[:], w.rearrange("(a p) m -> p a m", p=P))
-        x_sb = held.tile([P, KB, N], BF16, name="x_sb")
-        nc.sync.dma_start(x_sb[:], x.rearrange("(a p) n -> p a n", p=P))
+        nc.sync.dma_start(w_sb[:], w_blocks)
+        x_sb = [held.tile([P, N], BF16, name="x_sb%d" % a) for a in range(KB)]
+        for a in range(KB):
+            queue = nc.scalar if a % 2 == 0 else nc.sync
+            queue.dma_start(x_sb[a][:], x_blocks[:, a, :])
 
         ident = held.tile([P, P], BF16, name="ident")
         make_identity(nc, ident[:])
@@ -39,7 +42,7 @@ def tile_scatter_matmul_kernel(tc, base, x, w, offs, out):
             nc.tensor.matmul(
                 window[:].indirect(offsets[:]),
                 w_sb[:, a, :],
-                x_sb[:, a, :],
+                x_sb[a][:],
                 start=False,
                 stop=(a == KB - 1),
             )

@@ -8,6 +8,7 @@ S = 512
 N = 512
 K = 512
 KB = K // P
+WARM = 4
 
 FLOPS = 2 * K * P * N
 
@@ -31,6 +32,12 @@ def tile_scatter_matmul_kernel(tc, base, x, w, offs, out):
         for a in range(KB):
             queue = nc.scalar if a % 2 == 0 else nc.sync
             queue.dma_start(x_sb[a][:], x_blocks[:, a, :])
+
+        zeros = held.tile([P, N], BF16, name="zeros")
+        nc.vector.memset(zeros[:], 0.0)
+        idle_bank = psum.tile([P, N], F32, name="idle_bank")
+        for i in range(WARM):
+            nc.tensor.matmul(idle_bank[:], zeros[:, :P], zeros[:], start=True, stop=True)
 
         ident = held.tile([P, P], BF16, name="ident")
         make_identity(nc, ident[:])

@@ -22,16 +22,15 @@ def tile_scatter_matmul_kernel(tc, base, x, w, offs, out):
         w_blocks = w.rearrange("(p a) m -> p a m", a=KB)
         x_blocks = x.rearrange("(p a) n -> p a n", a=KB)
 
+        base_sb = held.tile([P, S], BF16, name="base_sb")
+        nc.sync.dma_start(base_sb[:], base)
         offsets = held.tile([P, N // 16], U16, name="offsets")
         nc.sync.dma_start(offsets[:], offs)
-        base_sb = held.tile([P, S], BF16, name="base_sb")
-        nc.scalar.dma_start(base_sb[:], base)
         w_sb = held.tile([P, KB, P], BF16, name="w_sb")
         nc.sync.dma_start(w_sb[:], w_blocks)
         x_sb = [held.tile([P, N], BF16, name="x_sb%d" % a) for a in range(KB)]
         for a in range(KB):
-            queue = nc.scalar if a % 2 == 0 else nc.sync
-            queue.dma_start(x_sb[a][:], x_blocks[:, a, :])
+            nc.sync.dma_start(x_sb[a][:], x_blocks[:, a, :])
 
         zeros = held.tile([P, N], BF16, name="zeros")
         nc.vector.memset(zeros[:], 0.0)

@@ -28,9 +28,10 @@ def tile_scatter_matmul_kernel(tc, base, x, w, offs, out):
         nc.sync.dma_start(offsets[:], offs)
         w_sb = held.tile([P, KB, P], BF16, name="w_sb")
         nc.sync.dma_start(w_sb[:], w_blocks)
-        x_sb = [held.tile([P, N], BF16, name="x_sb%d" % a) for a in range(KB)]
-        for a in range(KB):
-            nc.sync.dma_start(x_sb[a][:], x_blocks[:, a, :])
+        x_sb = held.tile([P, KB, N], BF16, name="x_sb")
+        nc.sync.dma_start(x_sb[:, 0, :], x_blocks[:, 0, :])
+        nc.sync.dma_start(x_sb[:, 1, :], x_blocks[:, 1, :])
+        nc.sync.dma_start(x_sb[:, 2:, :], x_blocks[:, 2:, :])
 
         zeros = held.tile([P, N], BF16, name="zeros")
         nc.vector.memset(zeros[:], 0.0)
@@ -48,11 +49,13 @@ def tile_scatter_matmul_kernel(tc, base, x, w, offs, out):
             nc.tensor.matmul(
                 window[:].indirect(offsets[:]),
                 w_sb[:, a, :],
-                x_sb[a][:],
+                x_sb[:, a, :],
                 start=False,
                 stop=(a == KB - 1),
             )
 
-        z_sb = held.tile([P, S], F32, name="z_sb")
-        nc.vector.tensor_copy(z_sb[:], window[:])
-        nc.sync.dma_start(out, z_sb[:])
+        for h in range(2):
+            cols = slice(h * (S // 2), (h + 1) * (S // 2))
+            z_sb = held.tile([P, S // 2], F32, name="z_sb%d" % h)
+            nc.vector.tensor_copy(z_sb[:], window[:, cols])
+            nc.sync.dma_start(out[:, cols], z_sb[:])

@@ -8,7 +8,7 @@ S = 512
 N = 512
 K = 512
 KB = K // P
-WARM = 4
+WARM = 2
 
 FLOPS = 2 * K * P * N
 

@@ -27,11 +27,12 @@ def tile_scatter_matmul_kernel(tc, base, x, w, offs, out):
         offsets = held.tile([P, N // 16], U16, name="offsets")
         nc.sync.dma_start(offsets[:], offs)
         w_sb = held.tile([P, KB, P], BF16, name="w_sb")
-        nc.sync.dma_start(w_sb[:], w_blocks)
         x_sb = held.tile([P, KB, N], BF16, name="x_sb")
+        nc.sync.dma_start(w_sb[:, 0, :], w_blocks[:, 0, :])
         nc.sync.dma_start(x_sb[:, 0, :], x_blocks[:, 0, :])
-        nc.sync.dma_start(x_sb[:, 1, :], x_blocks[:, 1, :])
-        nc.sync.dma_start(x_sb[:, 2:, :], x_blocks[:, 2:, :])
+        nc.sync.dma_start(w_sb[:, 1:, :], w_blocks[:, 1:, :])
+        for a in range(1, KB):
+            nc.sync.dma_start(x_sb[:, a, :], x_blocks[:, a, :])
 
         zeros = held.tile([P, N], BF16, name="zeros")
         nc.vector.memset(zeros[:], 0.0)

@@ -8,6 +8,7 @@ S = 512
 N = 512
 K = 512
 KB = K // P
+OUT_PIECES = 4
 WARM = 2
 
 FLOPS = 2 * K * P * N
@@ -28,10 +29,8 @@ def tile_scatter_matmul_kernel(tc, base, x, w, offs, out):
         nc.sync.dma_start(offsets[:], offs)
         w_sb = held.tile([P, KB, P], BF16, name="w_sb")
         x_sb = held.tile([P, KB, N], BF16, name="x_sb")
-        nc.sync.dma_start(w_sb[:, 0, :], w_blocks[:, 0, :])
-        nc.sync.dma_start(x_sb[:, 0, :], x_blocks[:, 0, :])
-        nc.sync.dma_start(w_sb[:, 1:, :], w_blocks[:, 1:, :])
-        for a in range(1, KB):
+        for a in range(KB):
+            nc.sync.dma_start(w_sb[:, a, :], w_blocks[:, a, :])
             nc.sync.dma_start(x_sb[:, a, :], x_blocks[:, a, :])
 
         zeros = held.tile([P, N], BF16, name="zeros")
@@ -55,8 +54,9 @@ def tile_scatter_matmul_kernel(tc, base, x, w, offs, out):
                 stop=(a == KB - 1),
             )
 
-        for h in range(2):
-            cols = slice(h * (S // 2), (h + 1) * (S // 2))
-            z_sb = held.tile([P, S // 2], F32, name="z_sb%d" % h)
+        store_queues = (nc.sync, nc.scalar)
+        for q in range(OUT_PIECES):
+            cols = slice(q * (S // OUT_PIECES), (q + 1) * (S // OUT_PIECES))
+            z_sb = held.tile([P, S // OUT_PIECES], F32, name="z_sb%d" % q)
             nc.vector.tensor_copy(z_sb[:], window[:, cols])
-            nc.sync.dma_start(out[:, cols], z_sb[:])
+            store_queues[q % 2].dma_start(out[:, cols], z_sb[:])

@@ -23,15 +23,18 @@ def tile_scatter_matmul_kernel(tc, base, x, w, offs, out):
         w_blocks = w.rearrange("(p a) m -> p a m", a=KB)
         x_blocks = x.rearrange("(p a) n -> p a n", a=KB)
 
-        base_sb = held.tile([P, S], BF16, name="base_sb")
-        nc.sync.dma_start(base_sb[:], base)
         offsets = held.tile([P, N // 16], U16, name="offsets")
         nc.sync.dma_start(offsets[:], offs)
+        base_sb = held.tile([P, S], BF16, name="base_sb")
+        nc.sync.dma_start(base_sb[:], base)
         w_sb = held.tile([P, KB, P], BF16, name="w_sb")
         x_sb = held.tile([P, KB, N], BF16, name="x_sb")
         for a in range(KB):
             nc.sync.dma_start(w_sb[:, a, :], w_blocks[:, a, :])
-            nc.sync.dma_start(x_sb[:, a, :], x_blocks[:, a, :])
+            x_pieces = 1 if a < KB // 2 else 2
+            for h in range(x_pieces):
+                cols = slice(h * (N // x_pieces), (h + 1) * (N // x_pieces))
+                nc.sync.dma_start(x_sb[:, a, cols], x_blocks[:, a, cols])
 
         zeros = held.tile([P, N], BF16, name="zeros")
         nc.vector.memset(zeros[:], 0.0)
@@ -54,7 +57,7 @@ def tile_scatter_matmul_kernel(tc, base, x, w, offs, out):
                 stop=(a == KB - 1),
             )
 
-        store_queues = (nc.sync, nc.scalar)
+        store_queues = (nc.scalar, nc.sync)
         for q in range(OUT_PIECES):
             cols = slice(q * (S // OUT_PIECES), (q + 1) * (S // OUT_PIECES))
             z_sb = held.tile([P, S // OUT_PIECES], F32, name="z_sb%d" % q)

@@ -20,8 +20,8 @@ def tile_scatter_matmul_kernel(tc, base, x, w, offs, out):
         tc.tile_pool(name="held", bufs=1) as held,
         tc.psum_pool(name="psum", bufs=1) as psum,
     ):
-        w_blocks = w.rearrange("(p a) m -> p a m", a=KB)
-        x_blocks = x.rearrange("(p a) n -> p a n", a=KB)
+        w_blocks = w.rearrange("(a p) m -> p a m", a=KB)
+        x_blocks = x.rearrange("(a p) n -> p a n", a=KB)
 
         offsets = held.tile([P, N // 16], U16, name="offsets")
         nc.sync.dma_start(offsets[:], offs)

@@ -23,10 +23,10 @@ def tile_scatter_matmul_kernel(tc, base, x, w, offs, out):
         w_blocks = w.rearrange("(a p) m -> p a m", a=KB)
         x_blocks = x.rearrange("(a p) n -> p a n", a=KB)
 
-        offsets = held.tile([P, N // 16], U16, name="offsets")
-        nc.sync.dma_start(offsets[:], offs)
         base_sb = held.tile([P, S], BF16, name="base_sb")
         nc.sync.dma_start(base_sb[:], base)
+        offsets = held.tile([P, N // 16], U16, name="offsets")
+        nc.sync.dma_start(offsets[:], offs)
         w_sb = held.tile([P, KB, P], BF16, name="w_sb")
         x_sb = held.tile([P, KB, N], BF16, name="x_sb")
         for a in range(KB):

import concourse.mybir as mybir
from concourse.masks import make_identity

BF16, F32, U16 = mybir.dt.bfloat16, mybir.dt.float32, mybir.dt.uint16

P = 128
S = 512
N = 512
K = 512
KB = K // P
OUT_PIECES = 4
WARM = 2

FLOPS = 2 * K * P * N


def tile_scatter_matmul_kernel(tc, base, x, w, offs, out):
    nc = tc.nc
    with (
        tc.tile_pool(name="held", bufs=1) as held,
        tc.psum_pool(name="psum", bufs=1) as psum,
    ):
        w_blocks = w.rearrange("(a p) m -> p a m", a=KB)
        x_blocks = x.rearrange("(a p) n -> p a n", a=KB)

        base_sb = held.tile([P, S], BF16, name="base_sb")
        nc.sync.dma_start(base_sb[:], base)
        offsets = held.tile([P, N // 16], U16, name="offsets")
        nc.sync.dma_start(offsets[:], offs)
        w_sb = held.tile([P, KB, P], BF16, name="w_sb")
        x_sb = held.tile([P, KB, N], BF16, name="x_sb")
        for a in range(KB):
            nc.sync.dma_start(w_sb[:, a, :], w_blocks[:, a, :])
            x_pieces = 1 if a < KB // 2 else 2
            for h in range(x_pieces):
                cols = slice(h * (N // x_pieces), (h + 1) * (N // x_pieces))
                nc.sync.dma_start(x_sb[:, a, cols], x_blocks[:, a, cols])

        zeros = held.tile([P, N], BF16, name="zeros")
        nc.vector.memset(zeros[:], 0.0)
        idle_bank = psum.tile([P, N], F32, name="idle_bank")
        for i in range(WARM):
            nc.tensor.matmul(idle_bank[:], zeros[:, :P], zeros[:], start=True, stop=True)

        ident = held.tile([P, P], BF16, name="ident")
        make_identity(nc, ident[:])

        window = psum.tile([P, S], F32, name="window")
        nc.tensor.matmul(window[:], ident[:], base_sb[:], start=True, stop=False)

        for a in range(KB):
            nc.tensor.matmul(
                window[:].indirect(offsets[:]),
                w_sb[:, a, :],
                x_sb[:, a, :],
                start=False,
                stop=(a == KB - 1),
            )

        store_queues = (nc.scalar, nc.sync)
        for q in range(OUT_PIECES):
            cols = slice(q * (S // OUT_PIECES), (q + 1) * (S // OUT_PIECES))
            z_sb = held.tile([P, S // OUT_PIECES], F32, name="z_sb%d" % q)
            nc.vector.tensor_copy(z_sb[:], window[:, cols])
            store_queues[q % 2].dma_start(out[:, cols], z_sb[:])
